import numpy as np, ml_dtypes
CORES = [113,118,241,246]
N = 4
BF = ml_dtypes.bfloat16
def f(rng, *shape):
    return (rng.standard_normal(shape, dtype=np.float32) * np.exp2(rng.integers(-2, 3, shape[:-1] + (1,)))).astype(BF)
def wide(rng, *shape):
    v = f(rng, *shape).astype(np.float32); k = shape[:-2] + (1, shape[-1])
    return (v * np.exp2(rng.integers(-6, 7, k)) * (rng.random(k) > 0.0625)).astype(BF)
def entries(a):
    return np.ascontiguousarray(a.T).reshape(-1)
def table(e):
    return np.ascontiguousarray(np.reshape(e, (-1, 16)).T).astype(np.int32)
def gentries(a):
    return np.ascontiguousarray(a.reshape(8, 16, -1).transpose(0, 2, 1)).reshape(8, -1)
def gtable(e):
    e = np.asarray(e); return np.ascontiguousarray(e.reshape(8, -1, 16).transpose(0, 2, 1)).reshape(128, -1).astype(np.int32)
GX, GY, GZ, P, S, CAP = 64, 32, 16, 8192, 6144, 512
B, NB, CELLS = P // 8, N * P // 8, (GX - 1) * (GY - 1) * (GZ - 1)
def coords(a):
    return np.ascontiguousarray(a.reshape(3, 16, -1).transpose(0, 2, 1)).reshape(3, -1)
def uncoords(v):
    return np.ascontiguousarray(v.reshape(3, -1, 16).transpose(0, 2, 1)).reshape(48, -1)
def corners(bm, c):
    g = np.arange(8)[:, None]; cx, cy, cz = c[0] + (g & 1), c[1] + (g >> 1 & 1), c[2] + (g >> 2)
    return bm[(cx >> 1) + (GX // 2) * ((cy >> 1) + (GY // 2) * (cz >> 1))] * 8 + (cx & 1) + 2 * (cy & 1) + 4 * (cz & 1)
def touch(bm, c):
    rk = corners(bm, c) // P
    return np.stack([(rk == q).any(axis=0) for q in range(N)])
def draw_map(rng):
    own = rng.permutation(np.repeat(np.arange(N), P // 512)).reshape(GZ // 8, GY // 8, GX // 8)
    own = np.repeat(np.repeat(np.repeat(own, 4, axis=0), 4, axis=1), 4, axis=2).reshape(-1); bm = np.zeros(NB, np.int64)
    for q in range(N): bm[own == q] = q * B + rng.permutation(B)
    return bm
def draw_cells(rng, t, r, first):
    c = rng.choice(np.flatnonzero(t[r] & (np.sum(t, axis=0) == 1)), S)
    m = np.concatenate([first, rng.integers(0, CELLS, rng.integers(N * CAP // 4, N * CAP // 2 + 1))]).astype(np.int64)
    far = t[:, m].copy(); far[r] = False
    m = m[((np.add.accumulate(far.astype(np.int64), axis=1) <= CAP) | ~far).all(axis=0)]; c[:len(m)] = m
    return rng.permutation(c)
def draw_go(rng, tc, r):
    e = []
    for q in range(N):
        a = np.flatnonzero(tc[q]) if q != r else np.zeros(0, np.int64); free = np.ones(S, bool); free[a] = False
        e.append(rng.permutation(np.concatenate([a, rng.permutation(np.flatnonzero(free))[:CAP - len(a)]])))
    return table(np.concatenate(e))
def draw_hit(rng, r, shape):
    q = (r + rng.integers(1, N, shape)) % N
    return np.where(rng.random(shape) < 0.5, rng.integers(0, S, shape), S + q * CAP + rng.integers(0, CAP, shape))
def draw(rng, kind):
    bm = draw_map(rng); cells = np.stack([a.reshape(-1) for a in np.meshgrid(np.arange(GX - 1), np.arange(GY - 1), np.arange(GZ - 1), indexing="ij")])
    t = touch(bm, cells); nt = np.sum(t, axis=0); pos, go, hit = [], [], []; z = rng.integers(0, N)
    for r in range(N):
        first = np.zeros(0, np.int64)
        if kind == "full":
            q = (r + 1) % N; first = rng.choice(np.flatnonzero(t[q] & (nt - t[q] - t[r] == 0)), CAP)
        if kind == "ends": first = np.array([0, CELLS - 1, (7 * (GY - 1) + 7) * (GZ - 1) + 7])
        c = draw_cells(rng, t, r, first); fr = rng.integers(0, 65536, (3, S)); h = draw_hit(rng, r, (8, P))
        if kind == "ends":
            fr = rng.choice(np.array([0, 1, 32768, 65535]), (3, S)); a, b = (1 if r == 0 else 0), (N - 2 if r == N - 1 else N - 1)
            edge = np.array([0, S - 1, S + a * CAP, S + a * CAP + CAP - 1, S + b * CAP, S + b * CAP + CAP - 1])
            for g in range(8): h[g, :6] = np.roll(edge, g); h[g, P - 6:] = np.roll(edge, -g)
        if kind == "alike":
            h[:, :P // 2] = draw_hit(rng, r, (1, P // 2)); h[:, P // 2:] = draw_hit(rng, r, (8, 1))
            if r == z: c = np.full(S, rng.choice(np.flatnonzero(t[r] & (nt == 1))))
        pos.append(uncoords((cells[:, c] + fr * 2.0 ** -16).astype(np.float32))); go.append(draw_go(rng, t[:, c], r)); hit.append(gtable(h))
    return {"pro": f(rng, N, 16, P), "bas": f(rng, N, 16, S), "pos": np.stack(pos), "alb": rng.random((N, 1, S), dtype=np.float32),
            "bmap": np.repeat(bm.reshape(1, 1, NB), N, axis=0).astype(np.int32), "go": np.stack(go), "hit": np.stack(hit)}
def setup_inputs(rng):
    return draw(rng, "")
def setup_inputs_full(rng):
    return draw(rng, "full")
def setup_inputs_ends(rng):
    d = draw(rng, "ends"); d["alb"] = np.where(rng.random((N, 1, S)) < 0.25, rng.integers(0, 2, (N, 1, S)), d["alb"]).astype(np.float32); return d
def setup_inputs_alike(rng):
    return draw(rng, "alike")
def setup_inputs_spread(rng):
    d = draw(rng, ""); d["pro"] = wide(rng, N, 16, P); d["bas"] = wide(rng, N, 16, S); return d
def check_inputs(d):
    bad = []
    try:
        x = np.stack([coords(a) for a in d["pos"]]); bm = d["bmap"].reshape(N, NB).astype(np.int64); e = np.stack([entries(a) for a in d["go"]]).reshape(N, N, CAP); h = np.stack([gentries(a) for a in d["hit"]])
        if not (np.isfinite(x).all() and (x >= 0).all() and (x < np.array([GX - 1, GY - 1, GZ - 1])[:, None]).all()): bad.append("pos")
        if not ((bm == bm[:1]).all() and np.array_equal(np.sort(bm[0]), np.arange(NB))): bad.append("bmap")
        if e.min() < 0 or e.max() >= S or (np.diff(np.sort(e, axis=2), axis=2) == 0).any(): bad.append("go")
        if h.min() < 0 or h.max() >= S + N * CAP or any(((h[r] >= S + r * CAP) & (h[r] < S + r * CAP + CAP)).any() for r in range(N)): bad.append("hit")
        if not all(np.isfinite(d[a].astype(np.float32)).all() for a in ("pro", "bas")): bad.append("finite")
        if not ((d["alb"] >= 0).all() and (d["alb"] <= 1).all()): bad.append("alb")
        if not bad:
            for r in range(N):
                t = touch(bm[0], np.floor(x[r]).astype(np.int64))
                for q in range(N):
                    if q != r and np.sum(t[q]) != np.sum(t[q, e[r, q]]) and "go_touch" not in bad: bad.append("go_touch")
    except Exception:
        bad.append("shape")
    return bad
def reference(pro, bas, pos, alb, bmap, go, hit):
    bm = bmap[0].reshape(-1).astype(np.int64); every = np.concatenate([a.astype(np.float64) for a in pro], axis=1); lit = np.zeros((N, 16, S), np.float64)
    for r in range(N):
        x = coords(pos[r]); c = np.floor(x).astype(np.int64); fr = (x - c.astype(np.float32)).astype(np.float64)
        num = corners(bm, c); b = bas[r].astype(np.float64); rad = np.zeros(S, np.float64)
        for g in range(8):
            w = (fr[0] if g & 1 else 1 - fr[0]) * (fr[1] if g & 2 else 1 - fr[1]) * (fr[2] if g & 4 else 1 - fr[2])
            rad += w * np.sum(every[:, num[g]] * b, axis=0)
        lit[r] = rad * alb[r, 0].astype(np.float64) * b
    y = np.zeros((N, 16, P), np.float64)
    for r in range(N):
        seen = np.concatenate([lit[r]] + [lit[q][:, entries(go[q])[r * CAP:(r + 1) * CAP]] for q in range(N)], axis=1); h = gentries(hit[r])
        for g in range(8): y[r] += seen[:, h[g]]
        y[r] = pro[r].astype(np.float64) + 0.125 * y[r]
    return {"y": y.astype(np.float32)}

from concourse.bass import DstId, RemoteDMATransfer
from concourse.mybir import AluOpType as A, ActivationFunctionType as F

S, P = 6144, 8192
NA = 448
NV = P // 8 - NA
CV, CA = NV // 16, NA // 16
W1 = 512
M2 = 25165824.0

f32, bf, i32, u16 = "float32", "bfloat16", "int32", "uint16"


def sb(text):
    out = {}
    for item in text.split():
        name, rows, cols, dtype = item.split(":")
        out[name] = ("sbuf", [int(rows), int(cols)], {"f": f32, "b": bf, "i": i32, "u": u16}[dtype])
    return out


SCRATCH = sb(
    "PC:128:1024:b BS:16:6144:b P48:48:384:f P16:16:1152:f BM:16:256:i GO:16:128:i AL:48:128:f HI:128:512:i "
    "PI:128:8:i PF:128:8:f P0:128:1:i IR:128:240:f I16:128:128:f IG:128:128:f IC:128:384:f IDB:128:128:b IDF:48:48:f "
    "QF:128:128:f QB:16:128:b BD:128:128:f B8:128:8:f ZW:16:240:f YW:128:136:f DUP:48:128:f CM:128:128:f CO:128:1:f "
    "ONE:128:128:f SEL:128:1024:f SR:36:1536:b E1:36:12:f E12:36:12:f RM:128:320:f "
    "T1S:128:1024:b TAB:128:4096:b TBB:128:4096:b BMF:16:256:f BMO:128:256:u "
    "BAS:128:6144:b EV:128:384:f EB:128:384:f OF1:128:384:u GG:128:3072:b SEEN:128:8192:f WE:128:144:f WT:128:144:f "
    "WN:128:144:f U1:128:144:f U0:128:144:f AB:128:48:f WZ:128:96:f WY:128:192:f W:128:384:f X:128:384:f SC:128:384:f "
    "R1:128:48:f R3:128:144:b RT:36:512:b X16:128:384:f "
    "GI:128:12:i GJ:128:36:i GK:128:24:i OG:128:12:u OC:128:24:u MK:128:192:f BC:128:192:b YM:128:192:f LC:128:192:f "
    "LIN:128:192:f "
    "HO:128:512:u")
SCRATCH.update({"PV": ("sbuf", [128, NV], bf), "PA": ("sbuf", [128, NA], bf), "HD": ("dram", [8, 128, CV], i32),
                "GF": ("sbuf", [16, 3, 8, 4], f32), "GA": ("sbuf", [128, 8 * NA], f32), "ACC": ("sbuf", [128, NV], f32),
                "YA": ("sbuf", [128, NA], f32)})
for _b in range(8):
    SCRATCH["PB%d" % _b] = ("psum", [128, 512], f32)

SEMAPHORES = ["sV", "sA", "sP", "sG", "dPC", "dBS", "dP48", "dP16", "dBM", "dGO", "dAL", "dH1", "dH2", "dPR",
              "dY1", "dY2", "sent1", "sent2", "arr", "arr1", "lin0", "lin1", "lin2"]


def bits(engines):
    m = 0
    for e in engines:
        m |= 1 << e
    return m


def masks(topo, src, dsts):
    far = [d for d in dsts if src not in topo.cores_of(d)]
    near = [d for d in dsts if d not in far]
    off = topo.engines(src, far[0])
    out = {}
    for n, d in enumerate(far):
        k = len(off) // len(far)
        out[d] = off[n * k:(n + 1) * k]
    for d in near:
        out[d] = [e for e in topo.engines(src, d) if e not in off]
    return out


def rank_program(g, core, T, topo):
    r = T.rank_of(core)
    if r is None:
        return
    cores = list(T.cores)
    others = [q for q in range(len(cores)) if q != r]
    queue = {"V": g.vector, "A": g.scalar, "P": g.tensor, "G": g, "S": g.sync}
    csem = {"V": "sV", "A": "sA", "P": "sP", "G": "sG"}
    total = {}
    waited = {e: {} for e in queue}
    writer, readers = {}, {}

    def wait(e, toks):
        need = {}
        for (_, s, n) in toks:
            need[s] = max(need.get(s, 0), n)
        for s, n in need.items():
            if waited[e].get(s, 0) < n:
                queue[e].wait_ge(T.sem[s], n)
                waited[e][s] = n

    def deps(e, rd, wr, dma):
        toks = [writer[k] for k in rd if k in writer]
        for k in wr:
            for t in ([writer[k]] if k in writer else []) + readers.get(k, []):
                if dma or t[0] != e:
                    toks.append(t)
        return toks

    def note(tok, rd, wr):
        for k in rd:
            readers.setdefault(k, []).append(tok)
        for k in wr:
            writer[k] = tok
            readers[k] = []

    def op(e, fn, rd=(), wr=()):
        wait(e, deps(e, rd, wr, False))
        s = csem[e]
        fn().then_inc(T.sem[s], 1)
        total[s] = total.get(s, 0) + 1
        note((e, s, total[s]), rd, wr)

    def dmas(e, s, pairs, rd=(), wr=()):
        wait(e, deps(e, rd, wr, True))
        for out, in_ in pairs:
            queue[e].dma_start(out, in_).then_inc(T.sem[s], 16)
        total[s] = total.get(s, 0) + 16 * len(pairs)
        note(("D", s, total[s]), rd, wr)

    V, ACT, PE = g.vector, g.scalar, g.tensor
    PB = [T["PB%d" % b] for b in range(8)]

    def ts(out, in0, s1, s2, op0, op1, rd, wr):
        if s2 is None:
            op("V", lambda: V.tensor_scalar(out, in0, s1, None, op0), rd, wr)
        else:
            op("V", lambda: V.tensor_scalar(out, in0, s1, s2, op0, op1), rd, wr)

    def tt(out, in0, in1, o, rd, wr):
        op("V", lambda: V.tensor_tensor(out, in0, in1, o), rd, wr)

    def cp(out, in_, rd, wr):
        op("V", lambda: V.tensor_copy(out, in_), rd, wr)

    def ms(ap, c, rd, wr):
        op("V", lambda: V.memset(ap, c), rd, wr)

    def act(out, in_, rd, wr):
        op("A", lambda: ACT.activation(out, in_, F.Copy), rd, wr)

    def mm(out, lhsT, rhs, rd, wr, start=True, stop=True):
        op("P", lambda: PE.matmul(out, lhsT, rhs, start, stop), rd, wr)

    def iota(out, pat, wr):
        op("G", lambda: g.iota(out, pat, 0, 0, allow_small_or_imprecise_dtypes=True), (), wr)

    dmas("S", "dPC", [(T.PC[:], T.pro[:])], wr=["PC"])
    dmas("S", "dP48", [(T.P48[:], T.pos[:])], wr=["P48"])
    dmas("S", "dP16", [(T.P16[:, 384 * a:384 * a + 384], T.pos[16 * a:16 * a + 16, :]) for a in range(3)], wr=["P16"])
    dmas("S", "dBS", [(T.BS[:], T.bas[:])], wr=["BS"])
    dmas("A", "dBM", [(T.BM[:], T.bmap[:])], wr=["BM"])
    dmas("A", "dAL", [(T.AL[:], T.alb[:])], wr=["AL"])
    dmas("A", "dGO", [(T.GO[:], T.go[:])], wr=["GO"])

    op("G", lambda: g.iota(T.P0[:], [[0, 1]], 0, 1), (), ["P0"])
    iota(T.IR[:], [[1, 240]], ["IR"])
    iota(T.I16[:], [[0, 8], [1, 16]], ["I16"])
    iota(T.IG[:], [[1, 8], [0, 16]], ["IG"])
    iota(T.IC[:, 0:128], [[0, 4], [16, 2], [1, 16]], ["IC0"])
    iota(T.IC[:, 128:256], [[16, 2], [0, 4], [1, 16]], ["IC1"])
    iota(T.IC[:, 256:320], [[16, 2], [0, 2], [1, 16]], ["IC2"])
    iota(T.IC[:, 320:384], [[16, 2], [0, 2], [1, 16]], ["IC3"])

    ms(T.PI[:], 0, [], ["PI"])
    ms(T.ONE[:], 1.0, [], ["ONE"])
    ms(T.RM[:], 1.0, [], ["RM"])
    cp(T.PI[:, 0:1], T.P0[:], ["P0", "PI"], ["PI0"])
    ts(T.PI[:, 1:2], T.P0[:], 15, None, A.bitwise_and, None, ["P0"], ["PI1"])
    ts(T.PI[:, 2:3], T.P0[:], 31, None, A.bitwise_and, None, ["P0"], ["PI2"])
    ts(T.PI[:, 3:4], T.P0[:], 4, None, A.arith_shift_right, None, ["P0"], ["PI3"])
    ts(T.PI[:, 4:5], T.P0[:], 4, 1, A.arith_shift_right, A.bitwise_and, ["P0"], ["PI4"])
    ms(T.RM[:, 0::8], 0.0, ["RM"], ["RM"])
    cp(T.PF[:], T.PI[:], ["PI0", "PI1", "PI2", "PI3", "PI4"], ["PF"])
    for n, c in enumerate([8.0, 1.0, 256.0, -4095.0]):
        ms(T.CO[32 * n:32 * n + 32, :], c, [], ["CO%d" % n])
    p_, pm, pm32, pg, pj = [T.PF[:, n:n + 1] for n in range(5)]
    ts(T.IDB[:], T.IR[:, 0:128], p_, None, A.is_equal, None, ["IR", "PF"], ["IDB"])
    ts(T.ZW[:], T.IR[0:16, :], -112.0, T.PF[0:16, 1:2], A.add, A.is_equal, ["IR", "PF"], ["ZW"])
    ts(T.IDF[:], T.IR[0:48, 0:48], T.PF[0:48, 0:1], None, A.is_equal, None, ["IR", "PF"], ["IDF"])
    ts(T.PF[:, 5:6], pm, 8.0, None, A.mult, None, ["PF"], ["PF5"])
    ts(T.QF[:], T.I16[:], pm, None, A.is_equal, None, ["I16", "PF"], ["QF"])
    for lo, hi, base in [(0, 32, 0.0), (32, 64, 32.0), (64, 128, 16.0)]:
        ts(T.DUP[:, lo:hi], T.I16[0:48, lo:hi], base, T.PF[0:48, 0:1], A.add, A.is_equal, ["I16", "PF"], ["DUP%d" % lo])
    tt(T.E1[:], T.IDF[0:36, 0:12], T.IDF[0:36, 12:24], A.add, ["IDF"], ["E1"])

    for j in range(8):
        mm(PB[j // 2][:, 128 * (j % 2):128 * (j % 2) + 128], T.PC[:, j::8], T.IDB[:], ["PC", "IDB"], ["B%d" % (j // 2)])
    for b in range(4):
        (act if b % 2 == 0 else cp)(T.T1S[:, 256 * b:256 * b + 256], PB[b][:, 0:256], [], ["B%d" % b, "T1%d" % b])
    tt(T.E12[:], T.E1[:], T.IDF[0:36, 24:36], A.add, ["IDF", "E1"], ["E12"])
    cp(T.BMF[:], T.BM[:], ["BM"], ["BMF"])
    for a in range(8):
        b = 4 + a // 2
        mm(PB[b][:, 128 * (a % 2):128 * (a % 2) + 128], T.T1S[:, a::8], T.IDB[:], ["T10", "T11", "T12", "T13", "IDB"], ["B%d" % b])
    for b in range(4):
        (act if b % 2 == 0 else cp)(T.TAB[:, 1024 * r + 256 * b:1024 * r + 256 * b + 256], PB[4 + b][:, 0:256], [],
                                    ["B%d" % (4 + b), "TAB%d" % b])

    eng = masks(topo, core, [cores[q] for q in others])
    near = [q for q in others if core in topo.cores_of(cores[q])][0]
    twin = [q for q in others if q != near and topo.die(cores[q]) == topo.die(core)][0]
    off, inner = topo.engines(core, cores[twin]), eng[cores[near]]

    def tr(q, engines, sem, src, dst):
        rid, pid = topo.addr(cores[q], core)
        return RemoteDMATransfer(dst_ids=[DstId(rid=rid, pnc=pid)], dma_engine_mask=bits(engines), remote_sem=T.sem[sem], src=src, dst=dst)

    def lands(q):
        return len(masks(topo, cores[q], [c for c in cores if c != cores[q]])[core])

    first, rest = T.TAB[:, 1024 * r:1024 * r + W1], T.TAB[:, 1024 * r + W1:1024 * r + 1024]
    handed = T.TAB[:, 1024 * twin:1024 * twin + W1]
    wait("G", deps("G", ["TAB%d" % b for b in range((W1 + 255) // 256)], [], True))
    g.remote_dma_fused([tr(twin, off, "arr1", first, first), tr(near, inner, "arr", first, first)], local_sem=T.sem.sent1)
    wait("G", deps("G", ["TAB%d" % b for b in range(4)], [], True))
    g.remote_dma_fused([tr(q, eng[cores[q]], "arr", rest, rest) for q in others], local_sem=T.sem.sent1)
    total["arr1"] = len(off)
    writer["TABt"] = ("D", "arr1", len(off))
    wait("G", [writer["TABt"]])
    g.remote_dma_fused([tr(near, inner, "arr", handed, handed)], local_sem=T.sem.sent1)
    total["sent1"] = 2 * len(off) + 3 * len(inner)
    total["arr"] = sum(lands(q) for q in others) + 2 * len(inner)
    writer["TABr"] = ("D", "arr", total["arr"])
    writer["sent"] = ("D", "sent1", total["sent1"])
    for a in range(8):
        op("G", lambda: g.affine_select(T.SEL[:, 128 * a:128 * a + 128], T.ONE[:], [[0, 8], [-1, 16]], A.is_equal, 0.0, -16 * a, 1),
           ["ONE"], ["SEL%d" % a])
    iota(T.SEEN[:, S + 512 * r:S + 512 * r + 512], [[0, 512]], ["SEENf%d" % r])

    dmas("S", "dH1", [(T.HD[a], T.hit[:, CV * a:CV * a + CV]) for a in range(8)], rd=["sent"], wr=["HD"])
    dmas("S", "dPR", [(T.HI[:, 8 * CV:512], T.hit[:, 8 * CV:512]), (T.PA[:], T.pro[:, 8 * NV:P])]
         + [(T.PV[16 * a:16 * a + 16, :], T.pro[:, NV * a:NV * a + NV]) for a in range(8)], wr=["HIa", "PA", "PV"])
    dmas("S", "dH2", [(T.HI[:, CV * k:CV * k + CV], T.HD[:, 16 * k:16 * k + 16, :]) for k in range(8)], rd=["HD"], wr=["HIv"])

    mm(PB[0][:, 0:384], T.DUP[:], T.P48[:], ["DUP0", "DUP32", "DUP64", "P48"], ["B0"])
    mm(PB[6][:, 0:256], T.QF[0:16, :], T.BMF[:], ["QF", "BMF"], ["B6"])
    for h in range(8):
        mm(PB[4][:, 0:144], T.ZW[:, 112 - 16 * h:240 - 16 * h], T.P16[:, h::8], ["ZW", "P16"], ["B4"], h == 0, h == 7)
    mm(PB[4][:, 144:192], T.AL[:], T.IDF[:], ["AL", "IDF"], ["B4"])
    cp(T.QB[:], T.QF[0:16, :], ["QF"], ["QB"])
    ts(T.BD[:], T.IG[:], pg, None, A.is_equal, None, ["IG", "PF"], ["BD"])
    ts(T.YW[:], T.IR[:, 0:136], -7.0, T.PF[:, 5:6], A.add, A.is_equal, ["IR", "PF5"], ["YW"])
    ts(T.EV[:], PB[0][:, 0:384], pj, M2, A.subtract, A.add, ["PF"], ["B0", "EV"])
    cp(T.B8[:], T.BD[:, 0::16], ["BD"], ["B8"])
    cp(T.BMO[:], PB[6][:, 0:256], [], ["B6", "BMO"])
    ts(T.EB[0:96, :], T.EV[0:96, :], -M2, None, A.add, None, ["EV"], ["EBa"])
    ts(T.EB[96:128, :], T.EV[96:128, :], -M2, 16.0, A.add, A.is_ge, ["EV"], ["EBb"])
    for n, (lo, hi) in enumerate([(0, 32), (32, 64), (64, 128)]):
        ts(T.CM[lo:hi, :], T.IC[lo:hi, 128 * n:128 * n + 128], T.PF[lo:hi, 2:3], T.CO[lo:hi, :], A.is_equal, A.mult,
           ["IC0", "IC1", "IC2", "IC3", "PF", "CO0", "CO1", "CO2", "CO3"], ["CM%d" % n])
    if r > 0:
        cp(T.GF[:, 0:r], T.GO[:, 0:32 * r], ["GO"], ["GFa"])
    if r < 3:
        cp(T.GF[:, r:3], T.GO[:, 32 * r + 32:128], ["GO"], ["GFb"])
    for n in range(12):
        op("A", lambda: ACT.activation(T.SR[:, 128 * n:128 * n + 128], T.ONE[0:36, :], F.Identity, scale=T.E12[:, n:n + 1]),
           ["ONE", "E12"], ["SR%d" % n])

    ts(T.WE[:], PB[4][:, 0:144], M2, -M2, A.add, A.add, [], ["B4", "WE"])
    ts(T.AB[:], PB[4][:, 144:192], 0.125, None, A.mult, None, [], ["B4", "AB"])
    tt(T.WT[:], PB[4][:, 0:144], T.WE[:], A.subtract, ["WE"], ["B4", "WT"])
    ts(T.WN[:], T.WT[:], -1.0, None, A.mult, None, ["WT"], ["WN"])
    tt(T.U1[:], T.WT[:], T.WN[:], A.max, ["WT", "WN"], ["U1"])
    ts(T.U0[:], T.U1[:], -1.0, 1.0, A.mult, A.add, ["U1"], ["U0"])

    bank = [7, 0, 1, 2, 3, 4]
    for n in range(6):
        c = 2 * n
        mm(PB[bank[n]][:], T.QB[:], T.BS[:, 512 * c:512 * c + 512], ["QB", "BS"], ["B%d" % bank[n]])
        act(T.BAS[:, 512 * c:512 * c + 512], PB[bank[n]][:], [], ["B%d" % bank[n], "BAS%d" % c])
    mm(PB[5][:, 0:384], T.CM[:], T.EB[:], ["CM0", "CM1", "CM2", "EBa", "EBb"], ["B5"])
    for a in range(8):
        mm(PB[6][:, 0:12], T.ZW[:, 112 - 16 * a:240 - 16 * a], T.GF[:, :, a, :], ["ZW", "GFa", "GFb"], ["B6"], a == 0, a == 7)
    for n in range(6):
        c = 2 * n + 1
        mm(PB[bank[n]][:], T.QB[:], T.BS[:, 512 * c:512 * c + 512], ["QB", "BS"], ["B%d" % bank[n]])

    U = [T.U0, T.U1]
    for z in range(2):
        tt(T.WZ[:, 48 * z:48 * z + 48], U[z][:, 96:144], T.AB[:], A.mult, ["U0", "U1", "AB"], ["WZ%d" % z])
    for n in range(4):
        tt(T.WY[:, 48 * n:48 * n + 48], U[n & 1][:, 48:96], T.WZ[:, 48 * (n >> 1):48 * (n >> 1) + 48], A.mult,
           ["WZ%d" % (n >> 1)], ["WY%d" % n])
    for j in range(8):
        tt(T.W[:, j::8], U[j & 1][:, 0:48], T.WY[:, 48 * (j >> 1):48 * (j >> 1) + 48], A.mult, ["WY%d" % (j >> 1)], ["W%d" % j])
    cp(T.OF1[:], PB[5][:, 0:384], [], ["B5", "OF1"])
    cp(T.GI[:], PB[6][:, 0:12], [], ["B6", "GI"])
    cp(T.OG[:], PB[6][:, 0:12], [], ["B6", "OG"])
    ts(T.GJ[:, 0:12], T.GI[:], 4, 1, A.arith_shift_right, A.bitwise_and, ["GI"], ["GJa"])
    ts(T.GJ[:, 12:24], T.GI[:], 5, None, A.arith_shift_right, None, ["GI"], ["GJb"])
    ts(T.GK[:, 12:24], T.GI[:], 15, None, A.bitwise_and, None, ["GI"], ["GKb"])
    ts(T.GJ[:, 24:36], T.GJ[:, 0:12], 192.0, None, A.mult, None, ["GJa"], ["GJc"])
    tt(T.GK[:, 0:12], T.GJ[:, 24:36], T.GJ[:, 12:24], A.add, ["GJb", "GJc"], ["GKa"])
    cp(T.OC[:], T.GK[:], ["GKa", "GKb"], ["OC"])

    tab = ["TAB0", "TAB1", "TAB2", "TAB3", "TABt", "TABr", "BMO"]
    cp(T.TBB[:, 0:2048], T.TAB[:].indirect(T.BMO[:, 0:128]), tab, ["TBa"])
    act(T.TBB[:, 2048:4096], T.TAB[:].indirect(T.BMO[:, 128:256]), tab, ["TBb"])

    tb = ["TBa", "TBb", "OF1"]
    allw = ["W%d" % j for j in range(8)]

    def dots(c, lo, hi, key):
        b = 5 if c < 10 else 6
        for t in range(4 * c + lo, 4 * c + hi):
            mm(PB[b][:, 8 * t % 320:8 * t % 320 + 8], T.SEEN[:, 128 * t:128 * t + 128], T.B8[:], [key, "B8"], ["B%d" % b])

    def weigh(b, lo, hi):
        tt(T.X[:, lo:hi], PB[b][:, 0:hi - lo], T.W[:, lo:hi], A.mult, allw, ["B%d" % b, "X%d" % b])

    def scan(b, lo, hi):
        op("V", lambda: V.tensor_tensor_scan(T.SC[:, lo:hi], T.RM[:, 0:hi - lo], T.X[:, lo:hi], 0.0, A.mult, A.add),
           ["RM", "X%d" % b], ["SC%d" % b])

    for n in range(6):
        c = 2 * n + 1
        act(T.GG[:, 512 * n:512 * n + 512], T.TBB[:].indirect(T.OF1[:, 32 * c:32 * c + 32]), tb, ["GG%d" % n])
    act(T.MK[:], T.QF[:, 0:16].indirect(T.OC[:, 12:24]), ["OC", "QF"], ["MK"])
    for c in range(12):
        cols = slice(512 * c, 512 * c + 512)
        n = c // 2
        b = bank[n]
        if c % 2 == 0:
            tt(T.SEEN[:, cols], T.TBB[:].indirect(T.OF1[:, 32 * c:32 * c + 32]), T.BAS[:, cols], A.mult,
               tb + ["BAS%d" % c], ["SEEN%d" % c])
            dots(c, 0, 4, "SEEN%d" % c)
        elif c < 11:
            tt(T.SEEN[:, cols], PB[b][:], T.GG[:, 512 * n:512 * n + 512], A.mult, ["GG%d" % n], ["B%d" % b, "SEEN%d" % c])
            act(T.BAS[:, cols], PB[b][:], [], ["B%d" % b, "BAS%d" % c])
            dots(c, 0, 4, "SEEN%d" % c)
        else:
            weigh(5, 0, 320)
            for h, key in enumerate(["SEEN11a", "SEEN11"]):
                tt(T.SEEN[:, 512 * c + 256 * h:512 * c + 256 * h + 256], PB[b][:, 256 * h:256 * h + 256],
                   T.GG[:, 512 * n + 256 * h:512 * n + 256 * h + 256], A.mult, ["GG%d" % n], ["B%d" % b, key])
                dots(c, 2 * h, 2 * h + 2, key)
            scan(5, 0, 320)
            act(T.BAS[:, cols], PB[b][:], [], ["B%d" % b, "BAS%d" % c])
    allbas = ["BAS%d" % c for c in range(12)]
    act(T.BC[:], T.BAS[:].indirect(T.OG[:]), allbas + ["OG"], ["BC"])
    weigh(6, 320, 384)
    scan(6, 320, 384)
    R, sc = T.SC[:, 7::8], ["SC5", "SC6"]
    for h in [0, 2, 4, 6, 1, 3, 5, 7]:
        b = 7 - h % 2
        mm(PB[b][:, h // 2:192:4], T.SEL[:, 128 * h:128 * h + 128], R, sc + ["SEL%d" % h], ["B%d" % b])
    act(T.X16[:, 0:192], PB[7][:, 0:192], [], ["B7", "X16a"])
    cp(T.R3[:, 0:48], R, sc, ["R3a"])
    tt(T.R1[:], R, T.R3[:, 0:48], A.subtract, sc + ["R3a"], ["R1"])
    cp(T.R3[:, 48:96], T.R1[:], ["R1"], ["R3b"])
    tt(T.R3[:, 96:144], T.R1[:], T.R3[:, 48:96], A.subtract, ["R1", "R3b"], ["R3c"])
    cp(T.X16[:, 192:384], PB[6][:, 0:192], [], ["B6", "X16b"])
    for t in range(4):
        mm(PB[0][0:36, 128 * t:128 * t + 128], T.R3[:, t::4], T.IDB[:], ["R3a", "R3b", "R3c"], ["B0"])
    act(T.RT[:], PB[0][0:36, :], [], ["B0", "RT"])

    tt(T.YM[:], T.X16[:].indirect(T.OC[:, 0:12]), T.MK[:], A.mult, ["X16a", "X16b", "OC", "MK"], ["YM"])
    mm(PB[7][:, 0:192], T.BD[:], T.YM[:], ["BD", "YM"], ["B7"])
    cp(T.HO[:, 0:256], T.HI[:, 0:256], ["HIa", "HIv"], ["HOa"])
    tt(T.LC[:], PB[7][:, 0:192], T.BC[:], A.mult, ["BC"], ["B7", "LC"])
    cp(T.HO[:, 256:512], T.HI[:, 256:512], ["HIa", "HIv"], ["HOb"])
    wait("G", deps("G", ["LC"], [], True))
    trs = []
    for n, q in enumerate(others):
        slot = [x for x in range(len(cores)) if x != q].index(r)
        trs.append(tr(q, eng[cores[q]], "lin%d" % slot, T.LC[:, 64 * n:64 * n + 64], T.LIN[:, 64 * slot:64 * slot + 64]))
        total["lin%d" % n] = lands(q)
        writer["LIN%d" % n] = ("D", "lin%d" % n, lands(q))
    g.remote_dma_fused(trs, local_sem=T.sem.sent2)
    total["sent2"] = len(off) + len(inner)

    order = sorted(range(3), key=lambda n: others[n] != near)

    def foreign(n, b, lo, hi, take):
        q = others[n]
        for a in range(lo, hi):
            mm(PB[b][:, 64 * a:64 * a + 64], T.SEL[:, 128 * a:128 * a + 128], T.LIN[:, 64 * n:64 * n + 64], ["LIN%d" % n], ["B%d" % b])
        take(T.SEEN[:, S + 512 * q + 64 * lo:S + 512 * q + 64 * hi], PB[b][:, 64 * lo:64 * hi], [], ["B%d" % b, "SEENf%d_%d" % (q, lo)])

    def unwrap(c):
        b = 1 + c % 5
        mm(PB[b][:], T.SR[:, 128 * c:128 * c + 128], T.RT[:], ["RT", "SR%d" % c], ["B%d" % b])

    for c in range(5):
        unwrap(c)
    for c in range(12):
        b = 1 + c % 5
        cols = slice(512 * c, 512 * c + 512)
        tt(T.SEEN[:, cols], PB[b][:], T.BAS[:, cols], A.mult, ["BAS%d" % c], ["B%d" % b, "SEEN%d" % c] + ["SEEN11a"] * (c == 11))
        if c + 5 < 12:
            unwrap(c + 5)
        if c == 4:
            foreign(order[0], 6, 0, 8, act)
        if c == 6:
            foreign(order[1], 7, 0, 8, act)
            foreign(order[2], 0, 0, 5, act)
    foreign(order[2], 4, 5, 8, cp)

    seen = [k for k in writer if k.startswith("SEEN")] + ["HOa", "HOb"]
    mm(PB[3][:, 0:NA], T.IDB[:], T.PA[:], ["PA"], ["B3"], True, False)
    for a in range(8):
        act(T.GA[:, NA * a:NA * a + NA], T.SEEN[:].indirect(T.HO[:, 8 * CV + CA * a:8 * CV + CA * a + CA]), seen, ["GA%d" % a])
        mm(PB[3][:, 0:NA], T.YW[:, 7 - a:135 - a], T.GA[:, NA * a:NA * a + NA], ["GA%d" % a, "YW"], ["B3"], False, a == 7)
    for k in range(8):
        for h in range(2):
            cols = slice(NV // 2 * h, NV // 2 * (h + 1))
            o = CV * k + CV // 2 * h
            tt(T.ACC[:, cols], T.SEEN[:].indirect(T.HO[:, o:o + CV // 2]), (T.ACC if k else T.PV)[:, cols], A.add,
               seen + ["PV", "ACC%d" % h], ["ACC%d" % h])
    act(T.YA[:], PB[3][:, 0:NA], [], ["B3", "YA"])
    dmas("S", "dY1", [(T.y[:, NV * a:NV * a + NV], T.ACC[16 * a:16 * a + 16, :]) for a in range(8)], rd=["ACC0", "ACC1"])
    dmas("A", "dY2", [(T.y[:, 8 * NV:P], T.YA[:])], rd=["YA"])
    wait("G", [("D", s, n) for s, n in total.items()])
